import numpy as np
import ml_dtypes


def mxq(x, axis, fmt="e4m3"):
    dtype, down = {"e4m3": (ml_dtypes.float8_e4m3fn, 7), "e5m2": (ml_dtypes.float8_e5m2, 14)}[fmt]
    v = np.moveaxis(np.asarray(x, np.float32).astype(ml_dtypes.bfloat16).astype(np.float64), axis, -1)
    blocks = v.reshape(v.shape[:-1] + (-1, 32))
    amax = np.abs(blocks).max(-1, keepdims=True)
    byte = np.maximum(np.where(amax > 0, np.frexp(amax)[1] - 1 + 127, 0) - down, 1)
    scale = np.exp2(byte - 127.0)
    codes = (blocks / scale).astype(np.float32).astype(dtype).astype(np.float64)
    return np.moveaxis((codes * scale).reshape(v.shape), -1, axis)


WIDE = False


def mx_kscale(k):
    if not WIDE:
        return np.ones(k)
    levels = np.array([10, -10, 5, -5, 0])
    if k % 512:
        return np.exp2(np.random.permutation(np.resize(levels, k // 32))).repeat(32)
    a = np.empty((k // 512, 16))
    for p in range(k // 512):
        a[p, :8] = np.random.permutation(np.resize(levels, 8))
        for g in range(8):
            far = levels[np.abs(levels - a[p, g]) >= 10]
            a[p, g + 8] = far[np.random.randint(len(far))]
    return np.exp2(a.ravel()).repeat(32)


def f64(x):
    return np.asarray(x).astype(np.float64)


def striped(idx):
    return np.tile(idx.reshape(-1, 16).T, (8, 1)).astype(np.uint16)


def unstriped(offs):
    return offs[:16].T.reshape(-1).astype(np.int64)


E2M1 = np.array([0.0, 0.5, 1.0, 1.5, 2.0, 3.0, 4.0, 6.0, -0.0, -0.5, -1.0, -1.5, -2.0, -3.0, -4.0, -6.0])


def pack_fp4(w):
    k, n = w.shape
    w = f64(np.asarray(w, np.float32).astype(ml_dtypes.bfloat16)).reshape(k // 32, 32, n)
    amax = np.abs(w).max(1)
    mant, ex = np.frexp(amax / 6.0)
    byte = np.clip(np.where(amax > 0, np.where(mant > 0.5, ex, ex - 1) + 127, 1), 1, 254)
    scaled = (w * np.exp2(127.0 - byte)[:, None, :]).reshape(k, n).astype(np.float32)
    c = np.ascontiguousarray(scaled.reshape(k // 512, 128, 4, n).transpose(0, 1, 3, 2)).astype(ml_dtypes.float4_e2m1fn).view(np.uint8) & 0xF
    words = (c[..., 0::2] | (c[..., 1::2] << 4)).reshape(k // 512, 128, 2 * n)
    return np.ascontiguousarray(words), np.ascontiguousarray(byte.astype(np.uint8).reshape(k // 512, 16, n))


def unpack_fp4(words, scales):
    g, _, n = scales.shape
    words = np.ascontiguousarray(words).reshape(g, 128, n, 2)
    nib = np.empty((g, 128, n, 4), np.uint8)
    nib[..., 0::2] = words & 0xF
    nib[..., 1::2] = words >> 4
    vals = E2M1[nib] * np.repeat(np.exp2(scales.astype(np.float64) - 127.0), 8, axis=1)[..., None]
    return vals.transpose(0, 1, 3, 2).reshape(g * 512, n)


def silu(v):
    return v / (1.0 + np.exp(-np.maximum(v, -700.0)))


K, T, S, V, H, N, J, U = 512, 2048, 1024, 512, 512, 128, 512, 1024


def setup_inputs():
    n = np.random.standard_normal
    s = mx_kscale(K)[:, None]
    u = mx_kscale(H)
    r = mx_kscale(J)[:, None]
    packed_w2 = pack_fp4(n((H, N)) / np.sqrt(2 * H) / u[:, None])
    return {
        "xT": (n((K, T)) * s).astype(np.float32),
        "aT": (n((J, U)) * r).astype(np.float32),
        "w1": (n((K, H)) / np.sqrt(K) / s * u).astype(np.float32),
        "w3": (n((J, H)) / np.sqrt(J) / r).astype(np.float32),
        "w2_words": packed_w2[0],
        "w2_scales": packed_w2[1],
        "offs": striped(np.random.permutation(T)[:S]),
        "pos1": striped(np.random.permutation(S)[:V]),
        "pos2": striped(np.random.permutation(S)[:V]),
    }


def reference(xT, aT, w1, w3, w2_words, w2_scales, offs, pos1, pos2):
    xq = mxq(f64(xT)[:, unstriped(offs)], 0, "e4m3")
    h = silu(mxq(f64(w1), 0, "e4m3").T @ xq)
    f = mxq(f64(w3), 0, "e4m3").T @ mxq(f64(aT), 0, "e4m3")
    z = h[:, unstriped(pos1)] * f[:, :V] + h[:, unstriped(pos2)] * f[:, V:2 * V]
    return silu(unpack_fp4(w2_words, w2_scales).T @ mxq(z, 0, "e4m3"))

@@ -1,0 +1,242 @@
+from contextlib import ExitStack
+
+import concourse.mybir as mybir
+
+K, T, S, V, H, N = 512, 2048, 1024, 512, 512, 128
+FLOPS = 2 * K * H * S + 2 * K * H * S + 2 * H * N * V
+
+F32 = mybir.dt.float32
+BF16 = mybir.dt.bfloat16
+I32 = mybir.dt.int32
+U32 = mybir.dt.uint32
+U16 = mybir.dt.uint16
+U8 = mybir.dt.uint8
+FP8X4 = mybir.dt.float8_e4m3fn_x4
+FP4X4 = mybir.dt.float4_e2m1fn_x4
+SILU = mybir.ActivationFunctionType.Silu
+MULT = mybir.AluOpType.mult
+ADD = mybir.AluOpType.add
+
+P = 128
+PACK = 4
+LANES = 16
+BANK = 512
+RUN = 4
+RING = 3
+
+X_CHUNKS = ((1024, 512, 512), (512, 512, 512, 256, 256))
+OUT_PIECES = (256, 128, 128)
+
+
+def tile_picked_dime_silu_e_kernel(
+    tc, xT, aT, w1, w3, w2_words, w2_scales, offs, pos1, pos2, out
+):
+    nc = tc.nc
+    with ExitStack() as ctx:
+        keep = ctx.enter_context(tc.tile_pool(name="keep", bufs=1))
+        psum = ctx.enter_context(tc.psum_pool(name="psum", bufs=1))
+
+        ring = [psum.tile([P, BANK], F32, name=f"bank{b}") for b in range(RING)]
+        taken = []
+
+        def next_bank():
+            taken.append(ring[len(taken) % RING])
+            return taken[-1]
+
+        def vector_copy(dst, src):
+            nc.vector.tensor_copy(out=dst, in_=src)
+
+        def scalar_copy(dst, src):
+            nc.scalar.copy(out=dst, in_=src)
+
+        def quantise(name, values):
+            width = values.shape[1] // PACK
+            codes = keep.tile([P, width], U32, name=name + "_codes", align_bytes=64)
+            scales = keep.tile([P, width], U8, name=name + "_scales", align_bytes=64)
+            nc.vector.quantize_mx(out=codes[:].bitcast(FP8X4), scales=scales[:], in_=values[:])
+            return codes, scales
+
+        x_rows = xT.rearrange("(p j) t -> p j t", j=PACK)
+        offs_sb = keep.tile([P, S // LANES], U16, name="offs_sb")
+        pos_sb = [keep.tile([P, V // LANES], U16, name=f"pos_sb{d}") for d in range(2)]
+        x_raw = []
+        for u in range(2):
+            c0 = 0
+            for width in X_CHUNKS[u]:
+                raw = keep.tile([P, 2, width], F32, name=f"x_raw{u}_{c0}")
+                nc.sync.dma_start(out=raw[:], in_=x_rows[:, 2 * u : 2 * u + 2, c0 : c0 + width])
+                if not x_raw:
+                    nc.sync.dma_start(offs_sb[:], offs)
+                x_raw.append((u, c0, width, raw))
+                c0 += width
+        w1_raw = keep.tile([P, PACK, H], F32, name="w1_raw")
+        nc.sync.dma_start(out=w1_raw[:], in_=w1.rearrange("(p j) c -> p j c", j=PACK))
+        w3_raw = keep.tile([P, PACK, H], F32, name="w3_raw")
+        nc.sync.dma_start(out=w3_raw[:], in_=w3.rearrange("(p j) c -> p j c", j=PACK))
+        a_rows = aT.rearrange("(p j) t -> p j t", j=PACK)
+        a_raw = []
+        for d, pos in enumerate((pos1, pos2)):
+            raw = keep.tile([P, PACK, V], F32, name=f"a_raw{d}")
+            nc.sync.dma_start(out=raw[:], in_=a_rows[:, :, d * V : (d + 1) * V])
+            nc.sync.dma_start(pos_sb[d][:], pos)
+            a_raw.append(raw)
+
+        w2_codes = keep.tile([P, 2 * N], U8, name="w2_codes", align_bytes=64)
+        w2_plane = keep.tile([P, N], U8, name="w2_plane", align_bytes=64)
+        nc.gpsimd.memset(w2_plane[:], 0)
+        nc.gpsimd.dma_start(out=w2_codes[:].bitcast(I32), in_=w2_words[0].bitcast(I32))
+        for q in range(4):
+            nc.gpsimd.dma_start(
+                out=w2_plane[32 * q : 32 * q + 4, :].bitcast(I32),
+                in_=w2_scales[0, 4 * q : 4 * q + 4, :].bitcast(I32),
+            )
+
+        pairs = [keep.tile([P, 2 * T], BF16, name=f"pairs{u}") for u in range(2)]
+        picked = [keep.tile([P, PACK * BANK], BF16, name=f"picked{s}", align_bytes=64) for s in range(2)]
+
+        def gather_pair(u, s):
+            dst = picked[s][:].bitcast(U32).rearrange("p (n u) -> p n u", u=2)[:, :, u]
+            cols = slice(s * BANK // LANES, (s + 1) * BANK // LANES)
+            nc.vector.tensor_copy(out=dst, in_=pairs[u][:].bitcast(U32).indirect(offs_sb[:, cols]))
+
+        for u, c0, width, raw in x_raw:
+            last = c0 + width == T
+            copy = vector_copy if u == 0 or last else scalar_copy
+            copy(
+                pairs[u][:, 2 * c0 : 2 * (c0 + width)].rearrange("p (c i e) -> p c e i", i=RUN, e=2),
+                raw[:].rearrange("p e (c i) -> p c e i", i=RUN),
+            )
+            if last:
+                gather_pair(u, 0)
+                gather_pair(u, 1)
+
+        def round_weights(name, raw, half, copy):
+            dealt = keep.tile([P, 2 * P * PACK], BF16, name=f"{name}_dealt{half}", align_bytes=64)
+            copy(
+                dealt[:].rearrange("p (t m j) -> p m j t", t=2, j=PACK),
+                raw[:].rearrange("p j (m t) -> p m j t", t=PACK)[:, :, :, 2 * half : 2 * half + 2],
+            )
+            return dealt
+
+        def round_angles(d, cols, copy):
+            width = cols.stop - cols.start
+            woven = keep.tile([P, PACK * width], BF16, name=f"a_woven{d}_{cols.start}", align_bytes=64)
+            copy(
+                woven[:].rearrange("p (c i j) -> p c j i", i=RUN, j=PACK),
+                a_raw[d][:, :, cols].rearrange("p j (c i) -> p c j i", i=RUN),
+            )
+            return woven
+
+        def product(acc, weights, t, moving):
+            codes, scales = weights[t // 2]
+            cols = slice((t % 2) * P, (t % 2 + 1) * P)
+            nc.tensor.matmul_mx(
+                out=acc,
+                lhsT=codes[:, cols].bitcast(FP8X4),
+                lhsT_scale=scales[:, cols],
+                rhs=moving[0][:].bitcast(FP8X4),
+                rhs_scale=moving[1][:],
+                start=True,
+                stop=True,
+            )
+
+        w1_dealt = [round_weights("w1", w1_raw, half, scalar_copy) for half in range(2)]
+        x_q = [quantise("x0", picked[0])]
+        w1_q = [quantise("w1_0", w1_dealt[0])]
+        x_q.append(quantise("x1", picked[1]))
+        w1_q.append(quantise("w1_1", w1_dealt[1]))
+        w3_dealt = [round_weights("w3", w3_raw, 0, scalar_copy), round_weights("w3", w3_raw, 1, vector_copy)]
+        w3_q = [quantise(f"w3_{half}", w3_dealt[half]) for half in range(2)]
+        a0_q = quantise("a0", round_angles(0, slice(0, V), vector_copy))
+
+        h = [keep.tile([P, S], F32, name=f"h{t}") for t in range(PACK)]
+        f_first = [keep.tile([P, V], F32, name=f"f_first{t}") for t in range(PACK)]
+        first = keep.tile([P, PACK, V], F32, name="first")
+
+        def message_tile(t):
+            for s in range(2):
+                acc = next_bank()
+                product(acc[:], w1_q, t, x_q[s])
+                nc.scalar.activation(out=h[t][:, s * BANK : (s + 1) * BANK], in_=acc[:], func=SILU)
+
+        def first_filter(t):
+            acc = next_bank()
+            product(acc[:], w3_q, t, a0_q)
+            scalar_copy(f_first[t][:], acc[:])
+
+        def first_term(t):
+            nc.vector.tensor_tensor(out=first[:, t, :], in0=h[t][:].indirect(pos_sb[0][:]), in1=f_first[t][:], op=MULT)
+
+        starts = [sum(OUT_PIECES[:n]) for n in range(len(OUT_PIECES))]
+        pieces = [slice(v0, v0 + width) for v0, width in zip(starts, OUT_PIECES)]
+
+        def second_filter(n, a_q):
+            width = OUT_PIECES[n]
+            f_second = keep.tile([P, PACK * width], F32, name=f"f_second{n}")
+            per_bank = BANK // width
+            for t0 in range(0, PACK, per_bank):
+                acc = next_bank()
+                for t in range(t0, t0 + per_bank):
+                    product(acc[:, (t - t0) * width : (t - t0 + 1) * width], w3_q, t, a_q)
+                scalar_copy(f_second[:, t0 * width : t0 * width + BANK], acc[:])
+            return f_second
+
+        for t in range(PACK - 1):
+            message_tile(t)
+        a1_woven = [round_angles(1, pieces[0], vector_copy)]
+        for t in range(PACK - 1):
+            first_filter(t)
+            first_term(t)
+        a1_woven += [round_angles(1, cols, scalar_copy) for cols in pieces[1:]]
+        message_tile(PACK - 1)
+        first_filter(PACK - 1)
+        a1_q = [quantise(f"a1_{n}", woven) for n, woven in enumerate(a1_woven)]
+        first_term(PACK - 1)
+        f_second = [second_filter(n, a1_q[n]) for n in range(len(pieces))]
+
+        second = [keep.tile([P, PACK, width], F32, name=f"second{n}") for n, width in enumerate(OUT_PIECES)]
+        z = [keep.tile([P, PACK * width], BF16, name=f"z{n}", align_bytes=64) for n, width in enumerate(OUT_PIECES)]
+
+        def second_term(n, t):
+            width = OUT_PIECES[n]
+            entries = slice(pieces[n].start // LANES, pieces[n].stop // LANES)
+            nc.vector.tensor_tensor(
+                out=second[n][:, t, :],
+                in0=h[t][:].indirect(pos_sb[1][:, entries]),
+                in1=f_second[n][:, t * width : (t + 1) * width],
+                op=MULT,
+            )
+
+        def add_terms(n):
+            nc.vector.tensor_tensor(
+                out=z[n][:].rearrange("p (c i t) -> p c t i", i=RUN, t=PACK),
+                in0=first[:, :, pieces[n]].rearrange("p t (c i) -> p c t i", i=RUN),
+                in1=second[n][:].rearrange("p t (c i) -> p c t i", i=RUN),
+                op=ADD,
+            )
+
+        def project(n):
+            z_codes, z_scales = quantise(f"z{n}", z[n])
+            acc = next_bank()[:, 0 : OUT_PIECES[n]]
+            nc.tensor.matmul_mx(
+                out=acc,
+                lhsT=w2_codes[:].bitcast(FP4X4),
+                lhsT_scale=w2_plane[:],
+                rhs=z_codes[:].bitcast(FP8X4),
+                rhs_scale=z_scales[:],
+                start=True,
+                stop=True,
+            )
+            result = keep.tile([P, OUT_PIECES[n]], F32, name=f"result{n}")
+            nc.scalar.activation(out=result[:], in_=acc, func=SILU)
+            nc.sync.dma_start(out=out[:, pieces[n]], in_=result[:])
+
+        for n in range(len(pieces)):
+            for t in range(PACK):
+                second_term(n, t)
+                if n > 0 and t == 0:
+                    add_terms(n - 1)
+                if n > 0 and t == 1:
+                    project(n - 1)
+        add_terms(len(pieces) - 1)
+        project(len(pieces) - 1)

@@ -1,6 +1,7 @@
 from contextlib import ExitStack
 
 import concourse.mybir as mybir
+from concourse.masks import make_identity
 
 K, T, S, V, H, N = 512, 2048, 1024, 512, 512, 128
 FLOPS = 2 * K * H * S + 2 * K * H * S + 2 * H * N * V
@@ -22,9 +23,11 @@ PACK = 4
 LANES = 16
 BANK = 512
 RUN = 4
-RING = 3
+RING = 4
 
-X_CHUNKS = ((1024, 512, 512), (512, 512, 512, 256, 256))
+X_CHUNKS = ((1024, 1024), (1024, 512, 512))
+A_SPLIT = 256
+MAIN = 384
 OUT_PIECES = (256, 128, 128)
 
 
@@ -38,6 +41,8 @@ def tile_picked_dime_silu_e_kernel(
 
         ring = [psum.tile([P, BANK], F32, name=f"bank{b}") for b in range(RING)]
         taken = []
+        ident = keep.tile([P, P], F32, name="ident")
+        make_identity(nc, ident[:])
 
         def next_bank():
             taken.append(ring[len(taken) % RING])
@@ -56,6 +61,8 @@ def tile_picked_dime_silu_e_kernel(
             nc.vector.quantize_mx(out=codes[:].bitcast(FP8X4), scales=scales[:], in_=values[:])
             return codes, scales
 
+        starts = [sum(OUT_PIECES[:n]) for n in range(len(OUT_PIECES))]
+        pieces = [slice(v0, v0 + width) for v0, width in zip(starts, OUT_PIECES)]
         x_rows = xT.rearrange("(p j) t -> p j t", j=PACK)
         offs_sb = keep.tile([P, S // LANES], U16, name="offs_sb")
         pos_sb = [keep.tile([P, V // LANES], U16, name=f"pos_sb{d}") for d in range(2)]
@@ -72,40 +79,49 @@ def tile_picked_dime_silu_e_kernel(
         w1_raw = keep.tile([P, PACK, H], F32, name="w1_raw")
         nc.sync.dma_start(out=w1_raw[:], in_=w1.rearrange("(p j) c -> p j c", j=PACK))
         w3_raw = keep.tile([P, PACK, H], F32, name="w3_raw")
-        nc.sync.dma_start(out=w3_raw[:], in_=w3.rearrange("(p j) c -> p j c", j=PACK))
         a_rows = aT.rearrange("(p j) t -> p j t", j=PACK)
         a_raw = []
         for d, pos in enumerate((pos1, pos2)):
             raw = keep.tile([P, PACK, V], F32, name=f"a_raw{d}")
             nc.sync.dma_start(out=raw[:], in_=a_rows[:, :, d * V : (d + 1) * V])
+            if d == 0:
+                nc.sync.dma_start(out=w3_raw[:], in_=w3.rearrange("(p j) c -> p j c", j=PACK))
             nc.sync.dma_start(pos_sb[d][:], pos)
             a_raw.append(raw)
 
         w2_codes = keep.tile([P, 2 * N], U8, name="w2_codes", align_bytes=64)
         w2_plane = keep.tile([P, N], U8, name="w2_plane", align_bytes=64)
-        nc.gpsimd.memset(w2_plane[:], 0)
-        nc.gpsimd.dma_start(out=w2_codes[:].bitcast(I32), in_=w2_words[0].bitcast(I32))
+        nc.vector.memset(w2_plane[:].bitcast(I32), 0)
+        nc.sync.dma_start(out=w2_codes[:].bitcast(I32), in_=w2_words[0].bitcast(I32))
         for q in range(4):
-            nc.gpsimd.dma_start(
+            nc.sync.dma_start(
                 out=w2_plane[32 * q : 32 * q + 4, :].bitcast(I32),
                 in_=w2_scales[0, 4 * q : 4 * q + 4, :].bitcast(I32),
             )
 
+        warm = keep.tile([P, 2], F32, name="warm")
+        nc.vector.memset(warm[:, 0:1], 0.0)
+        nc.scalar.activation(out=warm[:, 1:2], in_=warm[:, 0:1], func=SILU)
+
         pairs = [keep.tile([P, 2 * T], BF16, name=f"pairs{u}") for u in range(2)]
         picked = [keep.tile([P, PACK * BANK], BF16, name=f"picked{s}", align_bytes=64) for s in range(2)]
 
+        fetched = [keep.tile([P, 2 * BANK], U32, name=f"fetched{s}") for s in range(2)]
+
         def gather_pair(u, s):
-            dst = picked[s][:].bitcast(U32).rearrange("p (n u) -> p n u", u=2)[:, :, u]
+            dst = fetched[s][:, u * BANK : (u + 1) * BANK]
             cols = slice(s * BANK // LANES, (s + 1) * BANK // LANES)
             nc.vector.tensor_copy(out=dst, in_=pairs[u][:].bitcast(U32).indirect(offs_sb[:, cols]))
 
         for u, c0, width, raw in x_raw:
             last = c0 + width == T
-            copy = vector_copy if u == 0 or last else scalar_copy
-            copy(
-                pairs[u][:, 2 * c0 : 2 * (c0 + width)].rearrange("p (c i e) -> p c e i", i=RUN, e=2),
-                raw[:].rearrange("p e (c i) -> p c e i", i=RUN),
-            )
+            split = 0 if c0 == 0 else width * 5 // 8 if last else width
+            for b0, b1, copy in ((0, split, vector_copy), (split, width, scalar_copy)):
+                if b0 < b1:
+                    copy(
+                        pairs[u][:, 2 * (c0 + b0) : 2 * (c0 + b1)].rearrange("p (c i e) -> p c e i", i=RUN, e=2),
+                        raw[:, :, b0:b1].rearrange("p e (c i) -> p c e i", i=RUN),
+                    )
             if last:
                 gather_pair(u, 0)
                 gather_pair(u, 1)
@@ -118,13 +134,13 @@ def tile_picked_dime_silu_e_kernel(
             )
             return dealt
 
-        def round_angles(d, cols, copy):
-            width = cols.stop - cols.start
-            woven = keep.tile([P, PACK * width], BF16, name=f"a_woven{d}_{cols.start}", align_bytes=64)
-            copy(
-                woven[:].rearrange("p (c i j) -> p c j i", i=RUN, j=PACK),
-                a_raw[d][:, :, cols].rearrange("p j (c i) -> p c j i", i=RUN),
-            )
+        def round_angles(d, split):
+            woven = keep.tile([P, PACK * V], BF16, name=f"a_woven{d}", align_bytes=64)
+            for c0, c1, copy in ((0, split, vector_copy), (split, V, scalar_copy))[: 2 if split < V else 1]:
+                copy(
+                    woven[:, PACK * c0 : PACK * c1].rearrange("p (c i j) -> p c j i", i=RUN, j=PACK),
+                    a_raw[d][:, :, c0:c1].rearrange("p j (c i) -> p c j i", i=RUN),
+                )
             return woven
 
         def product(acc, weights, t, moving):
@@ -134,45 +150,55 @@ def tile_picked_dime_silu_e_kernel(
                 out=acc,
                 lhsT=codes[:, cols].bitcast(FP8X4),
                 lhsT_scale=scales[:, cols],
-                rhs=moving[0][:].bitcast(FP8X4),
-                rhs_scale=moving[1][:],
+                rhs=moving[0].bitcast(FP8X4),
+                rhs_scale=moving[1],
                 start=True,
                 stop=True,
             )
 
-        w1_dealt = [round_weights("w1", w1_raw, half, scalar_copy) for half in range(2)]
+        for s in range(2):
+            scalar_copy(
+                picked[s][:].bitcast(U32).rearrange("p (c i u) -> p c u i", i=RUN, u=2),
+                fetched[s][:].rearrange("p (u c i) -> p c u i", i=RUN, u=2),
+            )
+        w1_dealt = [round_weights("w1", w1_raw, 0, vector_copy), round_weights("w1", w1_raw, 1, scalar_copy)]
         x_q = [quantise("x0", picked[0])]
         w1_q = [quantise("w1_0", w1_dealt[0])]
         x_q.append(quantise("x1", picked[1]))
+        a0_woven = round_angles(0, V)
         w1_q.append(quantise("w1_1", w1_dealt[1]))
-        w3_dealt = [round_weights("w3", w3_raw, 0, scalar_copy), round_weights("w3", w3_raw, 1, vector_copy)]
-        w3_q = [quantise(f"w3_{half}", w3_dealt[half]) for half in range(2)]
-        a0_q = quantise("a0", round_angles(0, slice(0, V), vector_copy))
+        a0_q = quantise("a0", a0_woven)
+        w3_dealt = [round_weights("w3", w3_raw, 0, vector_copy)]
+        w3_q = [quantise("w3_0", w3_dealt[0])]
 
         h = [keep.tile([P, S], F32, name=f"h{t}") for t in range(PACK)]
-        f_first = [keep.tile([P, V], F32, name=f"f_first{t}") for t in range(PACK)]
+        f_first = [keep.tile([P, MAIN], F32, name=f"f_first{t}", align_bytes=64) for t in range(PACK)]
         first = keep.tile([P, PACK, V], F32, name="first")
 
         def message_tile(t):
             for s in range(2):
                 acc = next_bank()
-                product(acc[:], w1_q, t, x_q[s])
+                product(acc[:], w1_q, t, [part[:] for part in x_q[s]])
                 nc.scalar.activation(out=h[t][:, s * BANK : (s + 1) * BANK], in_=acc[:], func=SILU)
 
-        def first_filter(t):
+        def first_products(t):
             acc = next_bank()
-            product(acc[:], w3_q, t, a0_q)
-            scalar_copy(f_first[t][:], acc[:])
+            for cols in pieces[:-1]:
+                product(acc[:, cols], w3_q, t, [part[:, cols] for part in a0_q])
+            return acc[:, 0:MAIN]
 
-        def first_term(t):
-            nc.vector.tensor_tensor(out=first[:, t, :], in0=h[t][:].indirect(pos_sb[0][:]), in1=f_first[t][:], op=MULT)
+        def first_filter(t):
+            scalar_copy(f_first[t][:], first_products(t))
 
-        starts = [sum(OUT_PIECES[:n]) for n in range(len(OUT_PIECES))]
-        pieces = [slice(v0, v0 + width) for v0, width in zip(starts, OUT_PIECES)]
+        def first_term(t, cols, factor):
+            entries = slice(cols.start // LANES, cols.stop // LANES)
+            nc.vector.tensor_tensor(out=first[:, t, cols], in0=h[t][:].indirect(pos_sb[0][:, entries]), in1=factor, op=MULT)
 
-        def second_filter(n, a_q):
+
+        def second_filter(n, a_q, name):
             width = OUT_PIECES[n]
-            f_second = keep.tile([P, PACK * width], F32, name=f"f_second{n}")
+            a_q = [part[:, pieces[n]] for part in a_q]
+            f_second = keep.tile([P, PACK * width], F32, name=name)
             per_bank = BANK // width
             for t0 in range(0, PACK, per_bank):
                 acc = next_bank()
@@ -181,21 +207,27 @@ def tile_picked_dime_silu_e_kernel(
                 scalar_copy(f_second[:, t0 * width : t0 * width + BANK], acc[:])
             return f_second
 
-        for t in range(PACK - 1):
-            message_tile(t)
-        a1_woven = [round_angles(1, pieces[0], vector_copy)]
-        for t in range(PACK - 1):
+        message_tile(0)
+        w3_dealt.append(round_weights("w3", w3_raw, 1, scalar_copy))
+        message_tile(1)
+        early = keep.tile([P, MAIN], F32, name="early")
+        nc.vector.tensor_copy(out=early[:], in_=h[0][:].indirect(pos_sb[0][:, 0 : MAIN // LANES]))
+        w3_q.append(quantise("w3_1", w3_dealt[1]))
+        nc.vector.tensor_tensor(out=first[:, 0, 0:MAIN], in0=early[:], in1=first_products(0), op=MULT)
+        a1_woven = round_angles(1, A_SPLIT)
+        for t in range(1, PACK):
+            if t > 1:
+                message_tile(t)
             first_filter(t)
-            first_term(t)
-        a1_woven += [round_angles(1, cols, scalar_copy) for cols in pieces[1:]]
-        message_tile(PACK - 1)
-        first_filter(PACK - 1)
-        a1_q = [quantise(f"a1_{n}", woven) for n, woven in enumerate(a1_woven)]
-        first_term(PACK - 1)
-        f_second = [second_filter(n, a1_q[n]) for n in range(len(pieces))]
+            first_term(t, slice(0, MAIN), f_first[t][:])
+            if t == 1:
+                a1_q = quantise("a1", a1_woven)
+        f_second = [second_filter(n, a1_q, f"f_second{n}") for n in range(len(pieces) - 1)]
+        f_tail = second_filter(len(pieces) - 1, a0_q, "f_tail")
+        f_second.append(second_filter(len(pieces) - 1, a1_q, "f_second_tail"))
 
         second = [keep.tile([P, PACK, width], F32, name=f"second{n}") for n, width in enumerate(OUT_PIECES)]
-        z = [keep.tile([P, PACK * width], BF16, name=f"z{n}", align_bytes=64) for n, width in enumerate(OUT_PIECES)]
+        z = [keep.tile([P, PACK * width], BF16, name=f"z{n}", align_bytes=64) for n, width in enumerate(OUT_PIECES[:-1])]
 
         def second_term(n, t):
             width = OUT_PIECES[n]
@@ -217,7 +249,7 @@ def tile_picked_dime_silu_e_kernel(
 
         def project(n):
             z_codes, z_scales = quantise(f"z{n}", z[n])
-            acc = next_bank()[:, 0 : OUT_PIECES[n]]
+            acc = sums[n][:, 0 : OUT_PIECES[n]]
             nc.tensor.matmul_mx(
                 out=acc,
                 lhsT=w2_codes[:].bitcast(FP4X4),
@@ -231,12 +263,46 @@ def tile_picked_dime_silu_e_kernel(
             nc.scalar.activation(out=result[:], in_=acc, func=SILU)
             nc.sync.dma_start(out=out[:, pieces[n]], in_=result[:])
 
+        blocks = [(n, c0) for n in range(len(pieces) - 1) for c0 in range(0, OUT_PIECES[n], P)]
+        sums = [psum.tile([P, BANK], F32, name=f"sums{b}") for b in range(len(blocks))]
+
+        def add_transposed(b, t, term, opens, closes):
+            nc.tensor.matmul(
+                out=sums[b][:, t * P : (t + 1) * P], lhsT=term, rhs=ident[:], start=opens, stop=closes, is_transpose=True
+            )
+
+        def turn_back(b):
+            n, c0 = blocks[b]
+            rows = keep.tile([P, PACK * P], BF16, name=f"rows{b}")
+            scalar_copy(
+                rows[:].rearrange("v (u p e) -> v u p e", u=2, e=2),
+                sums[b][:].rearrange("v (u e p) -> v u p e", u=2, e=2),
+            )
+            turned = sums[b][:, 0 : 2 * P]
+            for u in range(2):
+                nc.tensor.transpose(turned[:, u * P : (u + 1) * P], rows[:].bitcast(F32)[:, u * P : (u + 1) * P], ident[:])
+            scalar_copy(
+                z[n][:].bitcast(F32)[:, 2 * c0 : 2 * (c0 + P)].rearrange("p (v u) -> p v u", u=2),
+                turned.rearrange("p (u v) -> p v u", u=2),
+            )
+
+        for b in range(len(blocks)):
+            for t in range(PACK):
+                add_transposed(b, t, first[:, t, b * P : (b + 1) * P], t == 0, False)
         for n in range(len(pieces)):
+            mine = [b for b in range(len(blocks)) if blocks[b][0] == n]
+            if not mine:
+                for t in range(PACK):
+                    first_term(t, pieces[n], f_tail[:, t * P : (t + 1) * P])
             for t in range(PACK):
                 second_term(n, t)
-                if n > 0 and t == 0:
-                    add_terms(n - 1)
-                if n > 0 and t == 1:
-                    project(n - 1)
+                for b in mine:
+                    c0 = blocks[b][1]
+                    add_transposed(b, t, second[n][:, t, c0 : c0 + P], False, t == PACK - 1)
+            for b in mine:
+                turn_back(b)
+        for n in range(len(pieces) - 1):
+            project(n)
+        z.append(keep.tile([P, PACK * OUT_PIECES[-1]], BF16, name="z0", align_bytes=64))
         add_terms(len(pieces) - 1)
         project(len(pieces) - 1)

@@ -23,12 +23,14 @@ PACK = 4
 LANES = 16
 BANK = 512
 RUN = 4
+QUADRANT = 32
 RING = 4
 
 X_CHUNKS = ((1024, 1024), (1024, 512, 512))
-A_SPLIT = 256
-MAIN = 384
 OUT_PIECES = (256, 128, 128)
+MAIN = sum(OUT_PIECES[:-1])
+TAIL = len(OUT_PIECES) - 1
+A_SPLIT = 256
 
 
 def tile_picked_dime_silu_e_kernel(
@@ -54,15 +56,20 @@ def tile_picked_dime_silu_e_kernel(
         def scalar_copy(dst, src):
             nc.scalar.copy(out=dst, in_=src)
 
-        def quantise(name, values):
-            width = values.shape[1] // PACK
+        def quantise(name, woven):
+            width = woven.shape[1] // PACK
             codes = keep.tile([P, width], U32, name=name + "_codes", align_bytes=64)
             scales = keep.tile([P, width], U8, name=name + "_scales", align_bytes=64)
-            nc.vector.quantize_mx(out=codes[:].bitcast(FP8X4), scales=scales[:], in_=values[:])
+            nc.vector.quantize_mx(out=codes[:].bitcast(FP8X4), scales=scales[:], in_=woven[:])
             return codes, scales
+
+        def entries(cols):
+            return slice(cols.start // LANES, cols.stop // LANES)
 
         starts = [sum(OUT_PIECES[:n]) for n in range(len(OUT_PIECES))]
         pieces = [slice(v0, v0 + width) for v0, width in zip(starts, OUT_PIECES)]
+        main = slice(0, MAIN)
+
         x_rows = xT.rearrange("(p j) t -> p j t", j=PACK)
         offs_sb = keep.tile([P, S // LANES], U16, name="offs_sb")
         pos_sb = [keep.tile([P, V // LANES], U16, name=f"pos_sb{d}") for d in range(2)]
@@ -77,25 +84,23 @@ def tile_picked_dime_silu_e_kernel(
                 x_raw.append((u, c0, width, raw))
                 c0 += width
         w1_raw = keep.tile([P, PACK, H], F32, name="w1_raw")
-        nc.sync.dma_start(out=w1_raw[:], in_=w1.rearrange("(p j) c -> p j c", j=PACK))
         w3_raw = keep.tile([P, PACK, H], F32, name="w3_raw")
+        a_raw = [keep.tile([P, PACK, V], F32, name=f"a_raw{d}") for d in range(2)]
         a_rows = aT.rearrange("(p j) t -> p j t", j=PACK)
-        a_raw = []
-        for d, pos in enumerate((pos1, pos2)):
-            raw = keep.tile([P, PACK, V], F32, name=f"a_raw{d}")
-            nc.sync.dma_start(out=raw[:], in_=a_rows[:, :, d * V : (d + 1) * V])
-            if d == 0:
-                nc.sync.dma_start(out=w3_raw[:], in_=w3.rearrange("(p j) c -> p j c", j=PACK))
-            nc.sync.dma_start(pos_sb[d][:], pos)
-            a_raw.append(raw)
+        nc.sync.dma_start(out=w1_raw[:], in_=w1.rearrange("(p j) c -> p j c", j=PACK))
+        nc.sync.dma_start(out=a_raw[0][:], in_=a_rows[:, :, 0:V])
+        nc.sync.dma_start(out=w3_raw[:], in_=w3.rearrange("(p j) c -> p j c", j=PACK))
+        nc.sync.dma_start(pos_sb[0][:], pos1)
+        nc.sync.dma_start(out=a_raw[1][:], in_=a_rows[:, :, V : 2 * V])
+        nc.sync.dma_start(pos_sb[1][:], pos2)
 
         w2_codes = keep.tile([P, 2 * N], U8, name="w2_codes", align_bytes=64)
-        w2_plane = keep.tile([P, N], U8, name="w2_plane", align_bytes=64)
-        nc.vector.memset(w2_plane[:].bitcast(I32), 0)
+        w2_scale_rows = keep.tile([P, N], U8, name="w2_scale_rows", align_bytes=64)
+        nc.vector.memset(w2_scale_rows[:].bitcast(I32), 0)
         nc.sync.dma_start(out=w2_codes[:].bitcast(I32), in_=w2_words[0].bitcast(I32))
-        for q in range(4):
+        for q in range(P // QUADRANT):
             nc.sync.dma_start(
-                out=w2_plane[32 * q : 32 * q + 4, :].bitcast(I32),
+                out=w2_scale_rows[QUADRANT * q : QUADRANT * q + 4, :].bitcast(I32),
                 in_=w2_scales[0, 4 * q : 4 * q + 4, :].bitcast(I32),
             )
 
@@ -105,26 +110,25 @@ def tile_picked_dime_silu_e_kernel(
 
         pairs = [keep.tile([P, 2 * T], BF16, name=f"pairs{u}") for u in range(2)]
         picked = [keep.tile([P, PACK * BANK], BF16, name=f"picked{s}", align_bytes=64) for s in range(2)]
-
         fetched = [keep.tile([P, 2 * BANK], U32, name=f"fetched{s}") for s in range(2)]
-
-        def gather_pair(u, s):
-            dst = fetched[s][:, u * BANK : (u + 1) * BANK]
-            cols = slice(s * BANK // LANES, (s + 1) * BANK // LANES)
-            nc.vector.tensor_copy(out=dst, in_=pairs[u][:].bitcast(U32).indirect(offs_sb[:, cols]))
-
         for u, c0, width, raw in x_raw:
-            last = c0 + width == T
-            split = 0 if c0 == 0 else width * 5 // 8 if last else width
-            for b0, b1, copy in ((0, split, vector_copy), (split, width, scalar_copy)):
-                if b0 < b1:
-                    copy(
-                        pairs[u][:, 2 * (c0 + b0) : 2 * (c0 + b1)].rearrange("p (c i e) -> p c e i", i=RUN, e=2),
-                        raw[:, :, b0:b1].rearrange("p e (c i) -> p c e i", i=RUN),
+            copy = scalar_copy if c0 == 0 else vector_copy
+            copy(
+                pairs[u][:, 2 * c0 : 2 * (c0 + width)].rearrange("p (c i e) -> p c e i", i=RUN, e=2),
+                raw[:].rearrange("p e (c i) -> p c e i", i=RUN),
+            )
+            if c0 + width == T:
+                for s in range(2):
+                    window = pairs[u][:].bitcast(U32)
+                    vector_copy(
+                        fetched[s][:, u * BANK : (u + 1) * BANK],
+                        window.indirect(offs_sb[:, entries(slice(s * BANK, (s + 1) * BANK))]),
                     )
-            if last:
-                gather_pair(u, 0)
-                gather_pair(u, 1)
+        for s in range(2):
+            scalar_copy(
+                picked[s][:].bitcast(U32).rearrange("p (c i u) -> p c u i", i=RUN, u=2),
+                fetched[s][:].rearrange("p (u c i) -> p c u i", i=RUN, u=2),
+            )
 
         def round_weights(name, raw, half, copy):
             dealt = keep.tile([P, 2 * P * PACK], BF16, name=f"{name}_dealt{half}", align_bytes=64)
@@ -134,141 +138,97 @@ def tile_picked_dime_silu_e_kernel(
             )
             return dealt
 
-        def round_angles(d, split):
+        def round_angles(d, shares):
             woven = keep.tile([P, PACK * V], BF16, name=f"a_woven{d}", align_bytes=64)
-            for c0, c1, copy in ((0, split, vector_copy), (split, V, scalar_copy))[: 2 if split < V else 1]:
+            for c0, c1, copy in shares:
                 copy(
                     woven[:, PACK * c0 : PACK * c1].rearrange("p (c i j) -> p c j i", i=RUN, j=PACK),
                     a_raw[d][:, :, c0:c1].rearrange("p j (c i) -> p c j i", i=RUN),
                 )
             return woven
 
-        def product(acc, weights, t, moving):
+        def product(acc, weights, t, moving, cols):
             codes, scales = weights[t // 2]
-            cols = slice((t % 2) * P, (t % 2 + 1) * P)
+            w_cols = slice((t % 2) * P, (t % 2 + 1) * P)
             nc.tensor.matmul_mx(
                 out=acc,
-                lhsT=codes[:, cols].bitcast(FP8X4),
-                lhsT_scale=scales[:, cols],
-                rhs=moving[0].bitcast(FP8X4),
-                rhs_scale=moving[1],
+                lhsT=codes[:, w_cols].bitcast(FP8X4),
+                lhsT_scale=scales[:, w_cols],
+                rhs=moving[0][:, cols].bitcast(FP8X4),
+                rhs_scale=moving[1][:, cols],
                 start=True,
                 stop=True,
             )
 
-        for s in range(2):
-            scalar_copy(
-                picked[s][:].bitcast(U32).rearrange("p (c i u) -> p c u i", i=RUN, u=2),
-                fetched[s][:].rearrange("p (u c i) -> p c u i", i=RUN, u=2),
-            )
         w1_dealt = [round_weights("w1", w1_raw, 0, vector_copy), round_weights("w1", w1_raw, 1, scalar_copy)]
         x_q = [quantise("x0", picked[0])]
         w1_q = [quantise("w1_0", w1_dealt[0])]
         x_q.append(quantise("x1", picked[1]))
-        a0_woven = round_angles(0, V)
+        a0_woven = round_angles(0, [(0, V, vector_copy)])
         w1_q.append(quantise("w1_1", w1_dealt[1]))
         a0_q = quantise("a0", a0_woven)
-        w3_dealt = [round_weights("w3", w3_raw, 0, vector_copy)]
-        w3_q = [quantise("w3_0", w3_dealt[0])]
+        w3_q = [quantise("w3_0", round_weights("w3", w3_raw, 0, vector_copy))]
 
         h = [keep.tile([P, S], F32, name=f"h{t}") for t in range(PACK)]
-        f_first = [keep.tile([P, MAIN], F32, name=f"f_first{t}", align_bytes=64) for t in range(PACK)]
         first = keep.tile([P, PACK, V], F32, name="first")
 
-        def message_tile(t):
+        def messages(t):
             for s in range(2):
                 acc = next_bank()
-                product(acc[:], w1_q, t, [part[:] for part in x_q[s]])
+                product(acc[:], w1_q, t, x_q[s], slice(0, BANK))
                 nc.scalar.activation(out=h[t][:, s * BANK : (s + 1) * BANK], in_=acc[:], func=SILU)
 
-        def first_products(t):
+        def main_filter(t):
             acc = next_bank()
-            for cols in pieces[:-1]:
-                product(acc[:, cols], w3_q, t, [part[:, cols] for part in a0_q])
-            return acc[:, 0:MAIN]
+            for cols in pieces[:TAIL]:
+                product(acc[:, cols], w3_q, t, a0_q, cols)
+            return acc[:, main]
 
-        def first_filter(t):
-            scalar_copy(f_first[t][:], first_products(t))
-
-        def first_term(t, cols, factor):
-            entries = slice(cols.start // LANES, cols.stop // LANES)
-            nc.vector.tensor_tensor(out=first[:, t, cols], in0=h[t][:].indirect(pos_sb[0][:, entries]), in1=factor, op=MULT)
-
-
-        def second_filter(n, a_q, name):
+        def piece_filter(name, a_q, n):
             width = OUT_PIECES[n]
-            a_q = [part[:, pieces[n]] for part in a_q]
-            f_second = keep.tile([P, PACK * width], F32, name=name)
+            held = keep.tile([P, PACK * width], F32, name=name)
             per_bank = BANK // width
             for t0 in range(0, PACK, per_bank):
                 acc = next_bank()
                 for t in range(t0, t0 + per_bank):
-                    product(acc[:, (t - t0) * width : (t - t0 + 1) * width], w3_q, t, a_q)
-                scalar_copy(f_second[:, t0 * width : t0 * width + BANK], acc[:])
-            return f_second
+                    product(acc[:, (t - t0) * width : (t - t0 + 1) * width], w3_q, t, a_q, pieces[n])
+                scalar_copy(held[:, t0 * width : t0 * width + BANK], acc[:])
+            return held
 
-        message_tile(0)
-        w3_dealt.append(round_weights("w3", w3_raw, 1, scalar_copy))
-        message_tile(1)
+        def term(dst, d, t, cols, factor):
+            nc.vector.tensor_tensor(out=dst, in0=h[t][:].indirect(pos_sb[d][:, entries(cols)]), in1=factor, op=MULT)
+
+        messages(0)
+        w3_late = round_weights("w3", w3_raw, 1, scalar_copy)
+        messages(1)
         early = keep.tile([P, MAIN], F32, name="early")
-        nc.vector.tensor_copy(out=early[:], in_=h[0][:].indirect(pos_sb[0][:, 0 : MAIN // LANES]))
-        w3_q.append(quantise("w3_1", w3_dealt[1]))
-        nc.vector.tensor_tensor(out=first[:, 0, 0:MAIN], in0=early[:], in1=first_products(0), op=MULT)
-        a1_woven = round_angles(1, A_SPLIT)
-        for t in range(1, PACK):
-            if t > 1:
-                message_tile(t)
-            first_filter(t)
-            first_term(t, slice(0, MAIN), f_first[t][:])
-            if t == 1:
-                a1_q = quantise("a1", a1_woven)
-        f_second = [second_filter(n, a1_q, f"f_second{n}") for n in range(len(pieces) - 1)]
-        f_tail = second_filter(len(pieces) - 1, a0_q, "f_tail")
-        f_second.append(second_filter(len(pieces) - 1, a1_q, "f_second_tail"))
+        vector_copy(early[:], h[0][:].indirect(pos_sb[0][:, entries(main)]))
+        w3_q.append(quantise("w3_1", w3_late))
+        nc.vector.tensor_tensor(out=first[:, 0, main], in0=early[:], in1=main_filter(0), op=MULT)
+        a1_woven = round_angles(1, [(0, A_SPLIT, vector_copy), (A_SPLIT, V, scalar_copy)])
+
+        def first_main_term(t):
+            factor = keep.tile([P, MAIN], F32, name=f"f_first{t}")
+            scalar_copy(factor[:], main_filter(t))
+            term(first[:, t, main], 0, t, main, factor[:])
+
+        first_main_term(1)
+        a1_q = quantise("a1", a1_woven)
+        for t in range(2, PACK):
+            messages(t)
+            first_main_term(t)
+        f_second = [piece_filter(f"f_second{n}", a1_q, n) for n in range(TAIL)]
+        f_first_tail = piece_filter("f_first_tail", a0_q, TAIL)
+        f_second.append(piece_filter("f_second_tail", a1_q, TAIL))
 
         second = [keep.tile([P, PACK, width], F32, name=f"second{n}") for n, width in enumerate(OUT_PIECES)]
-        z = [keep.tile([P, PACK * width], BF16, name=f"z{n}", align_bytes=64) for n, width in enumerate(OUT_PIECES[:-1])]
-
-        def second_term(n, t):
-            width = OUT_PIECES[n]
-            entries = slice(pieces[n].start // LANES, pieces[n].stop // LANES)
-            nc.vector.tensor_tensor(
-                out=second[n][:, t, :],
-                in0=h[t][:].indirect(pos_sb[1][:, entries]),
-                in1=f_second[n][:, t * width : (t + 1) * width],
-                op=MULT,
-            )
-
-        def add_terms(n):
-            nc.vector.tensor_tensor(
-                out=z[n][:].rearrange("p (c i t) -> p c t i", i=RUN, t=PACK),
-                in0=first[:, :, pieces[n]].rearrange("p t (c i) -> p c t i", i=RUN),
-                in1=second[n][:].rearrange("p t (c i) -> p c t i", i=RUN),
-                op=ADD,
-            )
-
-        def project(n):
-            z_codes, z_scales = quantise(f"z{n}", z[n])
-            acc = sums[n][:, 0 : OUT_PIECES[n]]
-            nc.tensor.matmul_mx(
-                out=acc,
-                lhsT=w2_codes[:].bitcast(FP4X4),
-                lhsT_scale=w2_plane[:],
-                rhs=z_codes[:].bitcast(FP8X4),
-                rhs_scale=z_scales[:],
-                start=True,
-                stop=True,
-            )
-            result = keep.tile([P, OUT_PIECES[n]], F32, name=f"result{n}")
-            nc.scalar.activation(out=result[:], in_=acc, func=SILU)
-            nc.sync.dma_start(out=out[:, pieces[n]], in_=result[:])
-
-        blocks = [(n, c0) for n in range(len(pieces) - 1) for c0 in range(0, OUT_PIECES[n], P)]
+        z = [keep.tile([P, PACK * OUT_PIECES[n]], BF16, name=f"z{n}", align_bytes=64) for n in range(TAIL)]
+        blocks = [(n, c0) for n in range(TAIL) for c0 in range(0, OUT_PIECES[n], P)]
         sums = [psum.tile([P, BANK], F32, name=f"sums{b}") for b in range(len(blocks))]
 
-        def add_transposed(b, t, term, opens, closes):
+        def add_transposed(b, t, values, opens, closes):
             nc.tensor.matmul(
-                out=sums[b][:, t * P : (t + 1) * P], lhsT=term, rhs=ident[:], start=opens, stop=closes, is_transpose=True
+                out=sums[b][:, t * P : (t + 1) * P], lhsT=values, rhs=ident[:], start=opens, stop=closes, is_transpose=True
             )
 
         def turn_back(b):
@@ -286,23 +246,50 @@ def tile_picked_dime_silu_e_kernel(
                 turned.rearrange("p (u v) -> p v u", u=2),
             )
 
+        def second_term(n, t):
+            width = OUT_PIECES[n]
+            term(second[n][:, t, :], 1, t, pieces[n], f_second[n][:, t * width : (t + 1) * width])
+
         for b in range(len(blocks)):
             for t in range(PACK):
                 add_transposed(b, t, first[:, t, b * P : (b + 1) * P], t == 0, False)
-        for n in range(len(pieces)):
-            mine = [b for b in range(len(blocks)) if blocks[b][0] == n]
-            if not mine:
-                for t in range(PACK):
-                    first_term(t, pieces[n], f_tail[:, t * P : (t + 1) * P])
+        for n in range(TAIL):
+            own = [b for b in range(len(blocks)) if blocks[b][0] == n]
             for t in range(PACK):
                 second_term(n, t)
-                for b in mine:
+                for b in own:
                     c0 = blocks[b][1]
                     add_transposed(b, t, second[n][:, t, c0 : c0 + P], False, t == PACK - 1)
-            for b in mine:
+            for b in own:
                 turn_back(b)
-        for n in range(len(pieces) - 1):
+        for t in range(PACK):
+            term(first[:, t, pieces[TAIL]], 0, t, pieces[TAIL], f_first_tail[:, t * P : (t + 1) * P])
+        for t in range(PACK):
+            second_term(TAIL, t)
+
+        def project(n):
+            z_codes, z_scales = quantise(f"z{n}", z[n])
+            acc = sums[n][:, 0 : OUT_PIECES[n]]
+            nc.tensor.matmul_mx(
+                out=acc,
+                lhsT=w2_codes[:].bitcast(FP4X4),
+                lhsT_scale=w2_scale_rows[:],
+                rhs=z_codes[:].bitcast(FP8X4),
+                rhs_scale=z_scales[:],
+                start=True,
+                stop=True,
+            )
+            result = keep.tile([P, OUT_PIECES[n]], F32, name=f"result{n}")
+            nc.scalar.activation(out=result[:], in_=acc, func=SILU)
+            nc.sync.dma_start(out=out[:, pieces[n]], in_=result[:])
+
+        for n in range(TAIL):
             project(n)
-        z.append(keep.tile([P, PACK * OUT_PIECES[-1]], BF16, name="z0", align_bytes=64))
-        add_terms(len(pieces) - 1)
-        project(len(pieces) - 1)
+        z.append(keep.tile([P, PACK * OUT_PIECES[TAIL]], BF16, name="z0", align_bytes=64))
+        nc.vector.tensor_tensor(
+            out=z[TAIL][:].rearrange("p (c i t) -> p c t i", i=RUN, t=PACK),
+            in0=first[:, :, pieces[TAIL]].rearrange("p t (c i) -> p c t i", i=RUN),
+            in1=second[TAIL][:].rearrange("p t (c i) -> p c t i", i=RUN),
+            op=ADD,
+        )
+        project(TAIL)

from contextlib import ExitStack

import concourse.mybir as mybir
from concourse.masks import make_identity

K, T, S, V, H, N = 512, 2048, 1024, 512, 512, 128
FLOPS = 2 * K * H * S + 2 * K * H * S + 2 * H * N * V

F32 = mybir.dt.float32
BF16 = mybir.dt.bfloat16
I32 = mybir.dt.int32
U32 = mybir.dt.uint32
U16 = mybir.dt.uint16
U8 = mybir.dt.uint8
FP8X4 = mybir.dt.float8_e4m3fn_x4
FP4X4 = mybir.dt.float4_e2m1fn_x4
SILU = mybir.ActivationFunctionType.Silu
MULT = mybir.AluOpType.mult
ADD = mybir.AluOpType.add

P = 128
PACK = 4
LANES = 16
BANK = 512
RUN = 4
QUADRANT = 32
RING = 4

X_CHUNKS = ((1024, 1024), (1024, 512, 512))
OUT_PIECES = (256, 128, 128)
MAIN = sum(OUT_PIECES[:-1])
TAIL = len(OUT_PIECES) - 1
A_SPLIT = 256


def tile_picked_dime_silu_e_kernel(
    tc, xT, aT, w1, w3, w2_words, w2_scales, offs, pos1, pos2, out
):
    nc = tc.nc
    with ExitStack() as ctx:
        keep = ctx.enter_context(tc.tile_pool(name="keep", bufs=1))
        psum = ctx.enter_context(tc.psum_pool(name="psum", bufs=1))

        ring = [psum.tile([P, BANK], F32, name=f"bank{b}") for b in range(RING)]
        taken = []
        ident = keep.tile([P, P], F32, name="ident")
        make_identity(nc, ident[:])

        def next_bank():
            taken.append(ring[len(taken) % RING])
            return taken[-1]

        def vector_copy(dst, src):
            nc.vector.tensor_copy(out=dst, in_=src)

        def scalar_copy(dst, src):
            nc.scalar.copy(out=dst, in_=src)

        def quantise(name, woven):
            width = woven.shape[1] // PACK
            codes = keep.tile([P, width], U32, name=name + "_codes", align_bytes=64)
            scales = keep.tile([P, width], U8, name=name + "_scales", align_bytes=64)
            nc.vector.quantize_mx(out=codes[:].bitcast(FP8X4), scales=scales[:], in_=woven[:])
            return codes, scales

        def entries(cols):
            return slice(cols.start // LANES, cols.stop // LANES)

        starts = [sum(OUT_PIECES[:n]) for n in range(len(OUT_PIECES))]
        pieces = [slice(v0, v0 + width) for v0, width in zip(starts, OUT_PIECES)]
        main = slice(0, MAIN)

        x_rows = xT.rearrange("(p j) t -> p j t", j=PACK)
        offs_sb = keep.tile([P, S // LANES], U16, name="offs_sb")
        pos_sb = [keep.tile([P, V // LANES], U16, name=f"pos_sb{d}") for d in range(2)]
        x_raw = []
        for u in range(2):
            c0 = 0
            for width in X_CHUNKS[u]:
                raw = keep.tile([P, 2, width], F32, name=f"x_raw{u}_{c0}")
                nc.sync.dma_start(out=raw[:], in_=x_rows[:, 2 * u : 2 * u + 2, c0 : c0 + width])
                if not x_raw:
                    nc.sync.dma_start(offs_sb[:], offs)
                x_raw.append((u, c0, width, raw))
                c0 += width
        w1_raw = keep.tile([P, PACK, H], F32, name="w1_raw")
        w3_raw = keep.tile([P, PACK, H], F32, name="w3_raw")
        a_raw = [keep.tile([P, PACK, V], F32, name=f"a_raw{d}") for d in range(2)]
        a_rows = aT.rearrange("(p j) t -> p j t", j=PACK)
        nc.sync.dma_start(out=w1_raw[:], in_=w1.rearrange("(p j) c -> p j c", j=PACK))
        nc.sync.dma_start(out=a_raw[0][:], in_=a_rows[:, :, 0:V])
        nc.sync.dma_start(out=w3_raw[:], in_=w3.rearrange("(p j) c -> p j c", j=PACK))
        nc.sync.dma_start(pos_sb[0][:], pos1)
        nc.sync.dma_start(out=a_raw[1][:], in_=a_rows[:, :, V : 2 * V])
        nc.sync.dma_start(pos_sb[1][:], pos2)

        w2_codes = keep.tile([P, 2 * N], U8, name="w2_codes", align_bytes=64)
        w2_scale_rows = keep.tile([P, N], U8, name="w2_scale_rows", align_bytes=64)
        nc.vector.memset(w2_scale_rows[:].bitcast(I32), 0)
        nc.sync.dma_start(out=w2_codes[:].bitcast(I32), in_=w2_words[0].bitcast(I32))
        for q in range(P // QUADRANT):
            nc.sync.dma_start(
                out=w2_scale_rows[QUADRANT * q : QUADRANT * q + 4, :].bitcast(I32),
                in_=w2_scales[0, 4 * q : 4 * q + 4, :].bitcast(I32),
            )

        warm = keep.tile([P, 2], F32, name="warm")
        nc.vector.memset(warm[:, 0:1], 0.0)
        nc.scalar.activation(out=warm[:, 1:2], in_=warm[:, 0:1], func=SILU)

        pairs = [keep.tile([P, 2 * T], BF16, name=f"pairs{u}") for u in range(2)]
        picked = [keep.tile([P, PACK * BANK], BF16, name=f"picked{s}", align_bytes=64) for s in range(2)]
        fetched = [keep.tile([P, 2 * BANK], U32, name=f"fetched{s}") for s in range(2)]
        for u, c0, width, raw in x_raw:
            copy = scalar_copy if c0 == 0 else vector_copy
            copy(
                pairs[u][:, 2 * c0 : 2 * (c0 + width)].rearrange("p (c i e) -> p c e i", i=RUN, e=2),
                raw[:].rearrange("p e (c i) -> p c e i", i=RUN),
            )
            if c0 + width == T:
                for s in range(2):
                    window = pairs[u][:].bitcast(U32)
                    vector_copy(
                        fetched[s][:, u * BANK : (u + 1) * BANK],
                        window.indirect(offs_sb[:, entries(slice(s * BANK, (s + 1) * BANK))]),
                    )
        for s in range(2):
            scalar_copy(
                picked[s][:].bitcast(U32).rearrange("p (c i u) -> p c u i", i=RUN, u=2),
                fetched[s][:].rearrange("p (u c i) -> p c u i", i=RUN, u=2),
            )

        def round_weights(name, raw, half, copy):
            dealt = keep.tile([P, 2 * P * PACK], BF16, name=f"{name}_dealt{half}", align_bytes=64)
            copy(
                dealt[:].rearrange("p (t m j) -> p m j t", t=2, j=PACK),
                raw[:].rearrange("p j (m t) -> p m j t", t=PACK)[:, :, :, 2 * half : 2 * half + 2],
            )
            return dealt

        def round_angles(d, shares):
            woven = keep.tile([P, PACK * V], BF16, name=f"a_woven{d}", align_bytes=64)
            for c0, c1, copy in shares:
                copy(
                    woven[:, PACK * c0 : PACK * c1].rearrange("p (c i j) -> p c j i", i=RUN, j=PACK),
                    a_raw[d][:, :, c0:c1].rearrange("p j (c i) -> p c j i", i=RUN),
                )
            return woven

        def product(acc, weights, t, moving, cols):
            codes, scales = weights[t // 2]
            w_cols = slice((t % 2) * P, (t % 2 + 1) * P)
            nc.tensor.matmul_mx(
                out=acc,
                lhsT=codes[:, w_cols].bitcast(FP8X4),
                lhsT_scale=scales[:, w_cols],
                rhs=moving[0][:, cols].bitcast(FP8X4),
                rhs_scale=moving[1][:, cols],
                start=True,
                stop=True,
            )

        w1_dealt = [round_weights("w1", w1_raw, 0, vector_copy), round_weights("w1", w1_raw, 1, scalar_copy)]
        x_q = [quantise("x0", picked[0])]
        w1_q = [quantise("w1_0", w1_dealt[0])]
        x_q.append(quantise("x1", picked[1]))
        a0_woven = round_angles(0, [(0, V, vector_copy)])
        w1_q.append(quantise("w1_1", w1_dealt[1]))
        a0_q = quantise("a0", a0_woven)
        w3_q = [quantise("w3_0", round_weights("w3", w3_raw, 0, vector_copy))]

        h = [keep.tile([P, S], F32, name=f"h{t}") for t in range(PACK)]
        first = keep.tile([P, PACK, V], F32, name="first")

        def messages(t):
            for s in range(2):
                acc = next_bank()
                product(acc[:], w1_q, t, x_q[s], slice(0, BANK))
                nc.scalar.activation(out=h[t][:, s * BANK : (s + 1) * BANK], in_=acc[:], func=SILU)

        def main_filter(t):
            acc = next_bank()
            for cols in pieces[:TAIL]:
                product(acc[:, cols], w3_q, t, a0_q, cols)
            return acc[:, main]

        def piece_filter(name, a_q, n):
            width = OUT_PIECES[n]
            held = keep.tile([P, PACK * width], F32, name=name)
            per_bank = BANK // width
            for t0 in range(0, PACK, per_bank):
                acc = next_bank()
                for t in range(t0, t0 + per_bank):
                    product(acc[:, (t - t0) * width : (t - t0 + 1) * width], w3_q, t, a_q, pieces[n])
                scalar_copy(held[:, t0 * width : t0 * width + BANK], acc[:])
            return held

        def term(dst, d, t, cols, factor):
            nc.vector.tensor_tensor(out=dst, in0=h[t][:].indirect(pos_sb[d][:, entries(cols)]), in1=factor, op=MULT)

        messages(0)
        w3_late = round_weights("w3", w3_raw, 1, scalar_copy)
        messages(1)
        early = keep.tile([P, MAIN], F32, name="early")
        vector_copy(early[:], h[0][:].indirect(pos_sb[0][:, entries(main)]))
        w3_q.append(quantise("w3_1", w3_late))
        nc.vector.tensor_tensor(out=first[:, 0, main], in0=early[:], in1=main_filter(0), op=MULT)
        a1_woven = round_angles(1, [(0, A_SPLIT, vector_copy), (A_SPLIT, V, scalar_copy)])

        def first_main_term(t):
            factor = keep.tile([P, MAIN], F32, name=f"f_first{t}")
            scalar_copy(factor[:], main_filter(t))
            term(first[:, t, main], 0, t, main, factor[:])

        first_main_term(1)
        a1_q = quantise("a1", a1_woven)
        for t in range(2, PACK):
            messages(t)
            first_main_term(t)
        f_second = [piece_filter(f"f_second{n}", a1_q, n) for n in range(TAIL)]
        f_first_tail = piece_filter("f_first_tail", a0_q, TAIL)
        f_second.append(piece_filter("f_second_tail", a1_q, TAIL))

        second = [keep.tile([P, PACK, width], F32, name=f"second{n}") for n, width in enumerate(OUT_PIECES)]
        z = [keep.tile([P, PACK * OUT_PIECES[n]], BF16, name=f"z{n}", align_bytes=64) for n in range(TAIL)]
        blocks = [(n, c0) for n in range(TAIL) for c0 in range(0, OUT_PIECES[n], P)]
        sums = [psum.tile([P, BANK], F32, name=f"sums{b}") for b in range(len(blocks))]

        def add_transposed(b, t, values, opens, closes):
            nc.tensor.matmul(
                out=sums[b][:, t * P : (t + 1) * P], lhsT=values, rhs=ident[:], start=opens, stop=closes, is_transpose=True
            )

        def turn_back(b):
            n, c0 = blocks[b]
            rows = keep.tile([P, PACK * P], BF16, name=f"rows{b}")
            scalar_copy(
                rows[:].rearrange("v (u p e) -> v u p e", u=2, e=2),
                sums[b][:].rearrange("v (u e p) -> v u p e", u=2, e=2),
            )
            turned = sums[b][:, 0 : 2 * P]
            for u in range(2):
                nc.tensor.transpose(turned[:, u * P : (u + 1) * P], rows[:].bitcast(F32)[:, u * P : (u + 1) * P], ident[:])
            scalar_copy(
                z[n][:].bitcast(F32)[:, 2 * c0 : 2 * (c0 + P)].rearrange("p (v u) -> p v u", u=2),
                turned.rearrange("p (u v) -> p v u", u=2),
            )

        def second_term(n, t):
            width = OUT_PIECES[n]
            term(second[n][:, t, :], 1, t, pieces[n], f_second[n][:, t * width : (t + 1) * width])

        for b in range(len(blocks)):
            for t in range(PACK):
                add_transposed(b, t, first[:, t, b * P : (b + 1) * P], t == 0, False)
        for n in range(TAIL):
            own = [b for b in range(len(blocks)) if blocks[b][0] == n]
            for t in range(PACK):
                second_term(n, t)
                for b in own:
                    c0 = blocks[b][1]
                    add_transposed(b, t, second[n][:, t, c0 : c0 + P], False, t == PACK - 1)
            for b in own:
                turn_back(b)
        for t in range(PACK):
            term(first[:, t, pieces[TAIL]], 0, t, pieces[TAIL], f_first_tail[:, t * P : (t + 1) * P])
        for t in range(PACK):
            second_term(TAIL, t)

        def project(n):
            z_codes, z_scales = quantise(f"z{n}", z[n])
            acc = sums[n][:, 0 : OUT_PIECES[n]]
            nc.tensor.matmul_mx(
                out=acc,
                lhsT=w2_codes[:].bitcast(FP4X4),
                lhsT_scale=w2_scale_rows[:],
                rhs=z_codes[:].bitcast(FP8X4),
                rhs_scale=z_scales[:],
                start=True,
                stop=True,
            )
            result = keep.tile([P, OUT_PIECES[n]], F32, name=f"result{n}")
            nc.scalar.activation(out=result[:], in_=acc, func=SILU)
            nc.sync.dma_start(out=out[:, pieces[n]], in_=result[:])

        for n in range(TAIL):
            project(n)
        z.append(keep.tile([P, PACK * OUT_PIECES[TAIL]], BF16, name="z0", align_bytes=64))
        nc.vector.tensor_tensor(
            out=z[TAIL][:].rearrange("p (c i t) -> p c t i", i=RUN, t=PACK),
            in0=first[:, :, pieces[TAIL]].rearrange("p t (c i) -> p c t i", i=RUN),
            in1=second[TAIL][:].rearrange("p t (c i) -> p c t i", i=RUN),
            op=ADD,
        )
        project(TAIL)
